import numpy as np
import ml_dtypes


def mxq(x, axis, fmt="e4m3"):
    dtype, down = {"e4m3": (ml_dtypes.float8_e4m3fn, 7), "e5m2": (ml_dtypes.float8_e5m2, 14)}[fmt]
    v = np.moveaxis(np.asarray(x, np.float32).astype(ml_dtypes.bfloat16).astype(np.float64), axis, -1)
    blocks = v.reshape(v.shape[:-1] + (-1, 32))
    amax = np.abs(blocks).max(-1, keepdims=True)
    byte = np.maximum(np.where(amax > 0, np.frexp(amax)[1] - 1 + 127, 0) - down, 1)
    scale = np.exp2(byte - 127.0)
    codes = (blocks / scale).astype(np.float32).astype(dtype).astype(np.float64)
    return np.moveaxis((codes * scale).reshape(v.shape), -1, axis)


WIDE = False


def mx_kscale(k, group=512):
    if not WIDE:
        return np.ones(k)
    levels = np.array([18, -18])
    if group != 512:
        return np.exp2(np.random.permutation(np.resize(levels, k // group))).repeat(group)
    if k % 512:
        return np.exp2(np.random.permutation(np.resize(levels, k // 32))).repeat(32)
    a = np.empty((k // 512, 16))
    for p in range(k // 512):
        a[p, :8] = np.random.permutation(np.resize(levels, 8))
        for g in range(8):
            far = levels[np.abs(levels - a[p, g]) >= 10]
            a[p, g + 8] = far[np.random.randint(len(far))]
    return np.exp2(a.ravel()).repeat(32)


def f64(x):
    return np.asarray(x).astype(np.float64)


G, D, M, O, N = 4, 128, 128, 128, 512


def setup_inputs():
    n = np.random.standard_normal
    s_d = mx_kscale(D, 0)
    s_o = mx_kscale(O, 0)
    return {
        "x": (n((G, D, N)) * s_d[:, None]).astype(np.float32),
        "w1": (n((G, D, M)) / np.sqrt(D) / s_d[:, None]).astype(np.float32),
        "w2": (n((G, D, M)) / np.sqrt(D) / s_d[:, None]).astype(np.float32),
        "fl": (np.random.uniform(0.05, 0.3, (G, M, 1))).astype(np.float32),
        "wo": (n((G, O, M)) / np.sqrt(O) / s_o[:, None]).astype(np.float32),
        "dy": (n((G, O, N)) * s_o[:, None]).astype(np.float32),
        "old": (0.3 * n((G, M, N))).astype(np.float32),
    }


def reference(x, w1, w2, fl, wo, dy, old):
    w1q = mxq(f64(w1), 1, "e4m3")
    xq = mxq(f64(x), 1, "e4m3")
    z1 = w1q.transpose(0, 2, 1) @ xq
    w2q = mxq(f64(w2), 1, "e4m3")
    z2 = w2q.transpose(0, 2, 1) @ xq
    e1 = np.exp(np.square(z1) * (-1.0))
    e2 = np.exp(np.square(z2) * (-1.0))
    woq = mxq(f64(wo), 1, "e4m3")
    dyq = mxq(f64(dy), 1, "e4m3")
    c0 = woq.transpose(0, 2, 1) @ dyq
    de1 = c0 * z2 / (e1 + e2 + f64(fl)) - c0 * z2 * e1 / np.square(e1 + e2 + f64(fl))
    dz1 = de1 * e1 * (-1.0) * z1 * 2.0
    y = dz1 + f64(old)
    return y

@@ -1,0 +1,240 @@
+from contextlib import ExitStack
+
+import concourse.mybir as mybir
+
+G, D, M, N = 4, 128, 128, 512
+FLOPS = 3 * 2 * G * D * M * N
+
+F32 = mybir.dt.float32
+BF16 = mybir.dt.bfloat16
+U32 = mybir.dt.uint32
+U8 = mybir.dt.uint8
+FP8X4 = mybir.dt.float8_e4m3fn_x4
+ACT = mybir.ActivationFunctionType
+ALU = mybir.AluOpType
+
+P = 128
+PACK = 4
+ROWS = D // PACK
+HALF = N // 2
+MM_N = 128
+
+
+def tile_rows_bgaussshare_kernel(tc, x, w1, w2, fl, wo, dy, old, out):
+    nc = tc.nc
+
+    with ExitStack() as ctx:
+        sb = ctx.enter_context(tc.tile_pool(name="sb", bufs=1))
+        ps = ctx.enter_context(tc.psum_pool(name="ps", bufs=1))
+        ctx.enter_context(tc.manual_schedule())
+
+        def by_partition(a):
+            return a.rearrange("g d n -> (g d) n").rearrange("(q j) n -> q j n", j=PACK)
+
+        def load(name, src, width):
+            raw = sb.tile([P, PACK, width], F32, name=name + "_raw")
+            nc.sync.dma_start(out=raw[:], in_=src)
+            return raw
+
+        def interleave(copy, name, raw_ap, width):
+            packed = sb.tile([P, width, PACK], BF16, name=name + "_bf", align_bytes=64)
+            copy(
+                out=packed[:].rearrange("p (c i) t -> p c t i", i=4),
+                in_=raw_ap.rearrange("p t (c i) -> p c t i", i=4),
+            )
+            return packed
+
+        def quantize(name, packed, width):
+            codes = sb.tile([P, width], U32, name=name + "_codes", align_bytes=64)
+            scales = sb.tile([P, width], U8, name=name + "_scales", align_bytes=64)
+            nc.vector.quantize_mx(
+                out=codes[:].bitcast(FP8X4),
+                scales=scales[:],
+                in_=packed[:].rearrange("p w j -> p (w j)"),
+            )
+            return codes, scales
+
+        def product(dst, g, weights, moving):
+            rows = slice(ROWS * g, ROWS * (g + 1))
+            for c in range(HALF // MM_N):
+                cols = slice(MM_N * c, MM_N * (c + 1))
+                nc.tensor.matmul_mx(
+                    out=dst[:, cols],
+                    lhsT=weights[0][rows, :].bitcast(FP8X4),
+                    lhsT_scale=weights[1][rows, :],
+                    rhs=moving[0][rows, cols].bitcast(FP8X4),
+                    rhs_scale=moving[1][rows, cols],
+                    start=True,
+                    stop=True,
+                )
+
+        halves = [slice(0, HALF), slice(HALF, N)]
+        z_bank = [ps.tile([P, 2 * HALF], F32, name="z%d" % g) for g in range(G)]
+        c_bank = [ps.tile([P, N], F32, name="c%d" % g) for g in range(G)]
+
+        fl_rows = sb.tile([P, P], F32, name="fl_rows", align_bytes=64)
+        fl_cols = sb.tile([P, P], F32, name="fl_cols", align_bytes=64)
+        nc.gpsimd.memset(fl_rows[:], 0.0)
+
+        x_hbm = by_partition(x)
+        x0_raw = load("x0", x_hbm[:, :, halves[0]], HALF)
+        w1_raw = load("w1", by_partition(w1), M)
+        w2_raw = load("w2", by_partition(w2), M)
+        nc.scalar.dma_start(
+            out=fl_rows[0:P:32, :].rearrange("b (g s) -> b g s", g=G),
+            in_=fl.rearrange("g (b s) o -> b g (s o)", s=32),
+        )
+        x1_raw = load("x1", x_hbm[:, :, halves[1]], HALF)
+        wo_raw = load("wo", by_partition(wo), M)
+        dy_raw = load("dy", by_partition(dy), N)
+        old_sb = sb.tile([P, G, N], F32, name="old_sb")
+        nc.sync.dma_start(out=old_sb[:], in_=old.rearrange("g m n -> m g n"))
+
+        floor = [fl_cols[:, 32 * g : 32 * g + 1] for g in range(G)]
+
+        x0_bf = interleave(nc.vector.tensor_copy, "x0", x0_raw[:], HALF)
+        w1_bf = interleave(nc.scalar.copy, "w1", w1_raw[:], M)
+        x0_q = quantize("x0", x0_bf, HALF)
+        w2_bf = interleave(nc.vector.tensor_copy, "w2", w2_raw[:], M)
+        w1_q = quantize("w1", w1_bf, M)
+        w2_q = quantize("w2", w2_bf, M)
+
+        def z_products(g, x_q):
+            product(z_bank[g][:, 0:HALF], g, w1_q, x_q)
+            product(z_bank[g][:, HALF:], g, w2_q, x_q)
+
+        for g in range(G):
+            z_products(g, x0_q)
+
+        nc.vector.transpose(fl_cols[:], fl_rows[:])
+        x1_bf = interleave(nc.vector.tensor_copy, "x1", x1_raw[:], HALF)
+        wo_bf = interleave(nc.vector.tensor_copy, "wo", wo_raw[:], M)
+        x1_q = quantize("x1", x1_bf, HALF)
+        wo_q = quantize("wo", wo_bf, M)
+
+        units = [(h, g) for h in range(2) for g in range(G)]
+        squares = {}
+        bells = {}
+        bell_sum = [sb.tile([P, N], F32, name="bell_sum%d" % g) for g in range(G)]
+        e1z1 = [sb.tile([P, N], F32, name="e1z1_%d" % g) for g in range(G)]
+        az2 = [sb.tile([P, N], F32, name="az2_%d" % g) for g in range(G)]
+        az2c = [sb.tile([P, N], F32, name="az2c_%d" % g) for g in range(G)]
+        numer = [sb.tile([P, N], F32, name="numer%d" % g) for g in range(G)]
+
+        def square(u):
+            h, g = units[u]
+            squares[u] = sb.tile([P, 2 * HALF], F32, name="sq%d" % u)
+            nc.scalar.activation(out=squares[u][:], in_=z_bank[g][:], func=ACT.Square)
+
+        def bell(u):
+            h, g = units[u]
+            bells[u] = sb.tile([P, 2 * HALF], F32, name="bell%d" % u)
+            nc.scalar.activation(out=bells[u][:], in_=squares[u][:], func=ACT.Exp, scale=-1.0)
+            nc.gpsimd.tensor_tensor(
+                out=bell_sum[g][:, halves[h]], in0=bells[u][:, 0:HALF], in1=bells[u][:, HALF:], op=ALU.add
+            )
+            nc.vector.tensor_tensor(
+                out=e1z1[g][:, halves[h]], in0=z_bank[g][:, 0:HALF], in1=bells[u][:, 0:HALF], op=ALU.mult
+            )
+            nc.vector.scalar_tensor_tensor(
+                out=az2[g][:, halves[h]],
+                in0=bells[u][:, HALF:],
+                scalar=floor[g],
+                in1=z_bank[g][:, HALF:],
+                op0=ALU.add,
+                op1=ALU.mult,
+            )
+            if h == 0:
+                z_products(g, x1_q)
+
+        dy_bf = {}
+
+        def dy_copy(h):
+            dy_bf[h] = interleave(nc.vector.tensor_copy, "dy%d" % h, dy_raw[:, :, halves[h]], HALF)
+
+        def dy_quant(h):
+            dy_q = quantize("dy%d" % h, dy_bf[h], HALF)
+            for g in range(G):
+                product(c_bank[g][:, halves[h]], g, wo_q, dy_q)
+
+        def times_c0(g):
+            nc.vector.scalar_tensor_tensor(
+                out=az2c[g][:], in0=az2[g][:], scalar=-2.0, in1=c_bank[g][:], op0=ALU.mult, op1=ALU.mult
+            )
+
+        def numerator(g):
+            nc.vector.tensor_tensor(out=numer[g][:], in0=az2c[g][:], in1=e1z1[g][:], op=ALU.mult)
+
+        extra = {
+            2: [lambda: dy_copy(0)],
+            3: [lambda: dy_copy(1)],
+            4: [lambda: dy_quant(0), lambda: dy_quant(1)],
+            5: [lambda: times_c0(0)],
+            6: [lambda: numerator(0)],
+        }
+        square(0)
+        for u in range(len(units)):
+            if u + 1 < len(units):
+                square(u + 1)
+            bell(u)
+            for f in extra.get(u, []):
+                f()
+        times_c0(1)
+        times_c0(2)
+        numerator(1)
+        times_c0(3)
+        numerator(2)
+        numerator(3)
+
+        s2 = {}
+        rinv = {}
+        rinv2 = {}
+        prod = {}
+        res = {}
+
+        def sum_square(g):
+            s2[g] = sb.tile([P, N], F32, name="s2_%d" % g)
+            nc.scalar.activation(out=s2[g][:], in_=bell_sum[g][:], func=ACT.Square, bias=floor[g])
+
+        def inv(g):
+            rinv[g] = sb.tile([P, N], F32, name="rinv%d" % g)
+            nc.scalar.activation(out=rinv[g][:], in_=s2[g][:], func=ACT.Abs_reciprocal_sqrt)
+
+        def inv_square(g, cols):
+            if g not in rinv2:
+                rinv2[g] = sb.tile([P, N], F32, name="rinv2_%d" % g)
+                prod[g] = sb.tile([P, N], F32, name="prod%d" % g)
+                res[g] = sb.tile([P, N], F32, name="res%d" % g)
+            nc.scalar.activation(out=rinv2[g][:, cols], in_=rinv[g][:, cols], func=ACT.Square)
+
+        def scale(g, cols):
+            nc.vector.tensor_tensor(out=prod[g][:, cols], in0=numer[g][:, cols], in1=rinv2[g][:, cols], op=ALU.mult)
+
+        def finish(g, cols):
+            nc.vector.tensor_tensor(out=res[g][:, cols], in0=prod[g][:, cols], in1=old_sb[:, g, cols], op=ALU.add)
+            nc.sync.dma_start(out=out[g, :, cols], in_=res[g][:, cols])
+
+        whole = slice(0, N)
+        sum_square(0)
+        inv(0)
+        sum_square(1)
+        inv_square(0, whole)
+        inv(1)
+        sum_square(2)
+        inv_square(1, whole)
+        inv(2)
+        sum_square(3)
+        inv_square(2, whole)
+        inv(3)
+        inv_square(3, halves[0])
+        inv_square(3, halves[1])
+        scale(0, whole)
+        scale(1, whole)
+        finish(0, whole)
+        finish(1, whole)
+        scale(2, whole)
+        finish(2, whole)
+        scale(3, halves[0])
+        scale(3, halves[1])
+        finish(3, halves[0])
+        finish(3, halves[1])

@@ -54,9 +54,9 @@ def tile_rows_bgaussshare_kernel(tc, x, w1, w2, fl, wo, dy, old, out):
             )
             return codes, scales
 
-        def product(dst, g, weights, moving):
+        def product(dst, g, weights, moving, width):
             rows = slice(ROWS * g, ROWS * (g + 1))
-            for c in range(HALF // MM_N):
+            for c in range(width // MM_N):
                 cols = slice(MM_N * c, MM_N * (c + 1))
                 nc.tensor.matmul_mx(
                     out=dst[:, cols],
@@ -69,50 +69,59 @@ def tile_rows_bgaussshare_kernel(tc, x, w1, w2, fl, wo, dy, old, out):
                 )
 
         halves = [slice(0, HALF), slice(HALF, N)]
-        z_bank = [ps.tile([P, 2 * HALF], F32, name="z%d" % g) for g in range(G)]
-        c_bank = [ps.tile([P, N], F32, name="c%d" % g) for g in range(G)]
+        whole = slice(0, N)
+        chunks = [slice(0, 128), slice(128, 256), slice(256, 512)]
+        widths = [c.stop - c.start for c in chunks]
+        banks = [[ps.tile([P, N], F32, name="bank%d_%d" % (b, g)) for g in range(G)] for b in range(2)]
+        c_bank = banks[1]
 
         fl_rows = sb.tile([P, P], F32, name="fl_rows", align_bytes=64)
         fl_cols = sb.tile([P, P], F32, name="fl_cols", align_bytes=64)
         nc.gpsimd.memset(fl_rows[:], 0.0)
 
         x_hbm = by_partition(x)
-        x0_raw = load("x0", x_hbm[:, :, halves[0]], HALF)
+        x0_raw = load("x0", x_hbm[:, :, chunks[0]], widths[0])
         w1_raw = load("w1", by_partition(w1), M)
         w2_raw = load("w2", by_partition(w2), M)
         nc.scalar.dma_start(
             out=fl_rows[0:P:32, :].rearrange("b (g s) -> b g s", g=G),
             in_=fl.rearrange("g (b s) o -> b g (s o)", s=32),
         )
-        x1_raw = load("x1", x_hbm[:, :, halves[1]], HALF)
         wo_raw = load("wo", by_partition(wo), M)
+        x1_raw = load("x1", x_hbm[:, :, chunks[1]], widths[1])
+        x2_raw = load("x2", x_hbm[:, :, chunks[2]], widths[2])
         dy_raw = load("dy", by_partition(dy), N)
         old_sb = sb.tile([P, G, N], F32, name="old_sb")
         nc.sync.dma_start(out=old_sb[:], in_=old.rearrange("g m n -> m g n"))
 
         floor = [fl_cols[:, 32 * g : 32 * g + 1] for g in range(G)]
+        x_q = {}
+        x_bf = {}
 
-        x0_bf = interleave(nc.vector.tensor_copy, "x0", x0_raw[:], HALF)
+        x_bf[0] = interleave(nc.vector.tensor_copy, "x0", x0_raw[:], widths[0])
         w1_bf = interleave(nc.scalar.copy, "w1", w1_raw[:], M)
-        x0_q = quantize("x0", x0_bf, HALF)
+        x_q[0] = quantize("x0", x_bf[0], widths[0])
         w2_bf = interleave(nc.vector.tensor_copy, "w2", w2_raw[:], M)
         w1_q = quantize("w1", w1_bf, M)
         w2_q = quantize("w2", w2_bf, M)
+        wo_bf = interleave(nc.scalar.copy, "wo", wo_raw[:], M)
 
-        def z_products(g, x_q):
-            product(z_bank[g][:, 0:HALF], g, w1_q, x_q)
-            product(z_bank[g][:, HALF:], g, w2_q, x_q)
+        def z_products(c, g):
+            w = widths[c]
+            product(banks[c % 2][g][:, 0:w], g, w1_q, x_q[c], w)
+            product(banks[c % 2][g][:, w : 2 * w], g, w2_q, x_q[c], w)
 
         for g in range(G):
-            z_products(g, x0_q)
+            z_products(0, g)
 
         nc.vector.transpose(fl_cols[:], fl_rows[:])
-        x1_bf = interleave(nc.vector.tensor_copy, "x1", x1_raw[:], HALF)
-        wo_bf = interleave(nc.vector.tensor_copy, "wo", wo_raw[:], M)
-        x1_q = quantize("x1", x1_bf, HALF)
+        x_bf[1] = interleave(nc.vector.tensor_copy, "x1", x1_raw[:], widths[1])
         wo_q = quantize("wo", wo_bf, M)
+        x_q[1] = quantize("x1", x_bf[1], widths[1])
+        for g in range(G):
+            z_products(1, g)
 
-        units = [(h, g) for h in range(2) for g in range(G)]
+        units = [(c, g) for c in range(3) for g in range(G)]
         squares = {}
         bells = {}
         bell_sum = [sb.tile([P, N], F32, name="bell_sum%d" % g) for g in range(G)]
@@ -122,55 +131,68 @@ def tile_rows_bgaussshare_kernel(tc, x, w1, w2, fl, wo, dy, old, out):
         numer = [sb.tile([P, N], F32, name="numer%d" % g) for g in range(G)]
 
         def square(u):
-            h, g = units[u]
-            squares[u] = sb.tile([P, 2 * HALF], F32, name="sq%d" % u)
-            nc.scalar.activation(out=squares[u][:], in_=z_bank[g][:], func=ACT.Square)
+            c, g = units[u]
+            w = widths[c]
+            squares[u] = sb.tile([P, 2 * w], F32, name="sq%d" % u)
+            nc.scalar.activation(out=squares[u][:], in_=banks[c % 2][g][:, 0 : 2 * w], func=ACT.Square)
 
         def bell(u):
-            h, g = units[u]
-            bells[u] = sb.tile([P, 2 * HALF], F32, name="bell%d" % u)
+            c, g = units[u]
+            w = widths[c]
+            z = banks[c % 2][g]
+            bells[u] = sb.tile([P, 2 * w], F32, name="bell%d" % u)
             nc.scalar.activation(out=bells[u][:], in_=squares[u][:], func=ACT.Exp, scale=-1.0)
             nc.gpsimd.tensor_tensor(
-                out=bell_sum[g][:, halves[h]], in0=bells[u][:, 0:HALF], in1=bells[u][:, HALF:], op=ALU.add
+                out=bell_sum[g][:, chunks[c]], in0=bells[u][:, 0:w], in1=bells[u][:, w:], op=ALU.add
             )
             nc.vector.tensor_tensor(
-                out=e1z1[g][:, halves[h]], in0=z_bank[g][:, 0:HALF], in1=bells[u][:, 0:HALF], op=ALU.mult
+                out=e1z1[g][:, chunks[c]], in0=z[:, 0:w], in1=bells[u][:, 0:w], op=ALU.mult
             )
             nc.vector.scalar_tensor_tensor(
-                out=az2[g][:, halves[h]],
-                in0=bells[u][:, HALF:],
+                out=az2[g][:, chunks[c]],
+                in0=bells[u][:, w:],
                 scalar=floor[g],
-                in1=z_bank[g][:, HALF:],
+                in1=z[:, w : 2 * w],
                 op0=ALU.add,
                 op1=ALU.mult,
             )
-            if h == 0:
-                z_products(g, x1_q)
 
         dy_bf = {}
+        dy_q = {}
+
+        def x2_copy():
+            x_bf[2] = interleave(nc.vector.tensor_copy, "x2", x2_raw[:], widths[2])
+
+        def x2_quant():
+            x_q[2] = quantize("x2", x_bf[2], widths[2])
 
         def dy_copy(h):
             dy_bf[h] = interleave(nc.vector.tensor_copy, "dy%d" % h, dy_raw[:, :, halves[h]], HALF)
 
         def dy_quant(h):
-            dy_q = quantize("dy%d" % h, dy_bf[h], HALF)
-            for g in range(G):
-                product(c_bank[g][:, halves[h]], g, wo_q, dy_q)
+            dy_q[h] = quantize("dy%d" % h, dy_bf[h], HALF)
+
+        def c_products(g):
+            for h in range(2):
+                product(c_bank[g][:, halves[h]], g, wo_q, dy_q[h], HALF)
 
         def times_c0(g):
             nc.vector.scalar_tensor_tensor(
                 out=az2c[g][:], in0=az2[g][:], scalar=-2.0, in1=c_bank[g][:], op0=ALU.mult, op1=ALU.mult
             )
 
-        def numerator(g):
-            nc.vector.tensor_tensor(out=numer[g][:], in0=az2c[g][:], in1=e1z1[g][:], op=ALU.mult)
+        def numerator(engine, g, cols):
+            engine.tensor_tensor(out=numer[g][:, cols], in0=az2c[g][:, cols], in1=e1z1[g][:, cols], op=ALU.mult)
 
         extra = {
-            2: [lambda: dy_copy(0)],
-            3: [lambda: dy_copy(1)],
-            4: [lambda: dy_quant(0), lambda: dy_quant(1)],
-            5: [lambda: times_c0(0)],
-            6: [lambda: numerator(0)],
+            0: [x2_copy],
+            1: [x2_quant] + [lambda: z_products(2, 0), lambda: z_products(2, 1)],
+            2: [lambda: z_products(2, 2)],
+            3: [lambda: z_products(2, 3)],
+            5: [lambda: dy_copy(0)],
+            7: [lambda: dy_copy(1)],
+            8: [lambda: dy_quant(0), lambda: dy_quant(1)] + [lambda g=g: c_products(g) for g in range(G)],
+            10: [lambda: times_c0(0)],
         }
         square(0)
         for u in range(len(units)):
@@ -179,26 +201,29 @@ def tile_rows_bgaussshare_kernel(tc, x, w1, w2, fl, wo, dy, old, out):
             bell(u)
             for f in extra.get(u, []):
                 f()
+        numerator(nc.gpsimd, 0, whole)
         times_c0(1)
+        numerator(nc.gpsimd, 1, halves[0])
         times_c0(2)
-        numerator(1)
         times_c0(3)
-        numerator(2)
-        numerator(3)
+        numerator(nc.vector, 1, halves[1])
+        numerator(nc.vector, 2, whole)
 
         s2 = {}
         rinv = {}
         rinv2 = {}
         prod = {}
         res = {}
+        half_prod = {}
 
-        def sum_square(g):
-            s2[g] = sb.tile([P, N], F32, name="s2_%d" % g)
-            nc.scalar.activation(out=s2[g][:], in_=bell_sum[g][:], func=ACT.Square, bias=floor[g])
+        def sum_square(g, cols):
+            if g not in s2:
+                s2[g] = sb.tile([P, N], F32, name="s2_%d" % g)
+                rinv[g] = sb.tile([P, N], F32, name="rinv%d" % g)
+            nc.scalar.activation(out=s2[g][:, cols], in_=bell_sum[g][:, cols], func=ACT.Square, bias=floor[g])
 
-        def inv(g):
-            rinv[g] = sb.tile([P, N], F32, name="rinv%d" % g)
-            nc.scalar.activation(out=rinv[g][:], in_=s2[g][:], func=ACT.Abs_reciprocal_sqrt)
+        def inv(g, cols):
+            nc.scalar.activation(out=rinv[g][:, cols], in_=s2[g][:, cols], func=ACT.Abs_reciprocal_sqrt)
 
         def inv_square(g, cols):
             if g not in rinv2:
@@ -207,6 +232,16 @@ def tile_rows_bgaussshare_kernel(tc, x, w1, w2, fl, wo, dy, old, out):
                 res[g] = sb.tile([P, N], F32, name="res%d" % g)
             nc.scalar.activation(out=rinv2[g][:, cols], in_=rinv[g][:, cols], func=ACT.Square)
 
+        def scale_inv(g, cols):
+            if g not in half_prod:
+                half_prod[g] = sb.tile([P, N], F32, name="half_prod%d" % g)
+                prod[g] = sb.tile([P, N], F32, name="prod%d" % g)
+                res[g] = sb.tile([P, N], F32, name="res%d" % g)
+            nc.vector.tensor_tensor(out=half_prod[g][:, cols], in0=numer[g][:, cols], in1=rinv[g][:, cols], op=ALU.mult)
+
+        def scale_again(g, cols):
+            nc.vector.tensor_tensor(out=prod[g][:, cols], in0=half_prod[g][:, cols], in1=rinv[g][:, cols], op=ALU.mult)
+
         def scale(g, cols):
             nc.vector.tensor_tensor(out=prod[g][:, cols], in0=numer[g][:, cols], in1=rinv2[g][:, cols], op=ALU.mult)
 
@@ -214,27 +249,33 @@ def tile_rows_bgaussshare_kernel(tc, x, w1, w2, fl, wo, dy, old, out):
             nc.vector.tensor_tensor(out=res[g][:, cols], in0=prod[g][:, cols], in1=old_sb[:, g, cols], op=ALU.add)
             nc.sync.dma_start(out=out[g, :, cols], in_=res[g][:, cols])
 
-        whole = slice(0, N)
-        sum_square(0)
-        inv(0)
-        sum_square(1)
-        inv_square(0, whole)
-        inv(1)
-        sum_square(2)
+        a, b = halves
+        sum_square(0, whole)
+        inv(0, whole)
+        sum_square(1, whole)
+        inv(1, whole)
+        sum_square(2, whole)
         inv_square(1, whole)
-        inv(2)
-        sum_square(3)
-        inv_square(2, whole)
-        inv(3)
-        inv_square(3, halves[0])
-        inv_square(3, halves[1])
-        scale(0, whole)
+        inv(2, a)
+        inv(2, b)
+        inv_square(2, a)
+        sum_square(3, a)
+        inv_square(2, b)
+        inv(3, a)
+        sum_square(3, b)
+        inv_square(3, a)
+        inv(3, b)
+        inv_square(3, b)
+        scale_inv(0, whole)
+        numerator(nc.vector, 3, whole)
+        scale_again(0, whole)
         scale(1, whole)
         finish(0, whole)
         finish(1, whole)
-        scale(2, whole)
+        scale(2, a)
+        scale(2, b)
         finish(2, whole)
-        scale(3, halves[0])
-        scale(3, halves[1])
-        finish(3, halves[0])
-        finish(3, halves[1])
+        scale(3, a)
+        finish(3, a)
+        scale(3, b)
+        finish(3, b)

@@ -36,8 +36,8 @@ def tile_rows_bgaussshare_kernel(tc, x, w1, w2, fl, wo, dy, old, out):
             nc.sync.dma_start(out=raw[:], in_=src)
             return raw
 
-        def interleave(copy, name, raw_ap, width):
-            packed = sb.tile([P, width, PACK], BF16, name=name + "_bf", align_bytes=64)
+        def interleave(copy, name, raw_ap, width, tag=""):
+            packed = sb.tile([P, width, PACK], BF16, name=name + "_bf", tag=tag, align_bytes=64)
             copy(
                 out=packed[:].rearrange("p (c i) t -> p c t i", i=4),
                 in_=raw_ap.rearrange("p t (c i) -> p c t i", i=4),
@@ -75,46 +75,52 @@ def tile_rows_bgaussshare_kernel(tc, x, w1, w2, fl, wo, dy, old, out):
         banks = [[ps.tile([P, N], F32, name="bank%d_%d" % (b, g)) for g in range(G)] for b in range(2)]
         c_bank = banks[1]
 
-        fl_rows = sb.tile([P, P], F32, name="fl_rows", align_bytes=64)
-        fl_cols = sb.tile([P, P], F32, name="fl_cols", align_bytes=64)
-        nc.gpsimd.memset(fl_rows[:], 0.0)
+        fl_sb = sb.tile([P, G, 8], F32, name="fl_sb")
+        nc.scalar.dma_start(out=fl_sb[:, :, 0:1], in_=fl.rearrange("g m o -> m g o"))
 
         x_hbm = by_partition(x)
         x0_raw = load("x0", x_hbm[:, :, chunks[0]], widths[0])
         w1_raw = load("w1", by_partition(w1), M)
         w2_raw = load("w2", by_partition(w2), M)
-        nc.scalar.dma_start(
-            out=fl_rows[0:P:32, :].rearrange("b (g s) -> b g s", g=G),
-            in_=fl.rearrange("g (b s) o -> b g (s o)", s=32),
-        )
         wo_raw = load("wo", by_partition(wo), M)
         x1_raw = load("x1", x_hbm[:, :, chunks[1]], widths[1])
         x2_raw = load("x2", x_hbm[:, :, chunks[2]], widths[2])
-        dy_raw = load("dy", by_partition(dy), N)
+        dy_hbm = by_partition(dy)
+        dy_raw = [load("dy%d" % h, dy_hbm[:, :, halves[h]], HALF) for h in range(2)]
         old_sb = sb.tile([P, G, N], F32, name="old_sb")
         nc.sync.dma_start(out=old_sb[:], in_=old.rearrange("g m n -> m g n"))
 
-        floor = [fl_cols[:, 32 * g : 32 * g + 1] for g in range(G)]
+        floor = [fl_sb[:, g, 0:1] for g in range(G)]
         x_q = {}
         x_bf = {}
 
-        x_bf[0] = interleave(nc.vector.tensor_copy, "x0", x0_raw[:], widths[0])
-        w1_bf = interleave(nc.scalar.copy, "w1", w1_raw[:], M)
-        x_q[0] = quantize("x0", x_bf[0], widths[0])
-        w2_bf = interleave(nc.vector.tensor_copy, "w2", w2_raw[:], M)
-        w1_q = quantize("w1", w1_bf, M)
-        w2_q = quantize("w2", w2_bf, M)
-        wo_bf = interleave(nc.scalar.copy, "wo", wo_raw[:], M)
+        def z_product(c, g, s):
+            w = widths[c]
+            product(banks[c % 2][g][:, s * w : (s + 1) * w], g, w_q[s], x_q[c], w)
 
         def z_products(c, g):
-            w = widths[c]
-            product(banks[c % 2][g][:, 0:w], g, w1_q, x_q[c], w)
-            product(banks[c % 2][g][:, w : 2 * w], g, w2_q, x_q[c], w)
+            z_product(c, g, 0)
+            z_product(c, g, 1)
 
+        w_q = {}
+        first_squares = sb.tile([P, G, 2, widths[0]], F32, name="first_squares")
+
+        def first_square(g, s):
+            w = widths[0]
+            nc.scalar.activation(out=first_squares[:, g, s], in_=banks[0][g][:, s * w : (s + 1) * w], func=ACT.Square)
+
+        x_bf[0] = interleave(nc.vector.tensor_copy, "x0", x0_raw[:], widths[0])
+        w1_bf = interleave(nc.vector.tensor_copy, "w1", w1_raw[:], M)
+        x_q[0] = quantize("x0", x_bf[0], widths[0])
+        w_q[0] = quantize("w1", w1_bf, M)
         for g in range(G):
-            z_products(0, g)
-
-        nc.vector.transpose(fl_cols[:], fl_rows[:])
+            z_product(0, g, 0)
+            first_square(g, 0)
+        w2_bf = interleave(nc.vector.tensor_copy, "w2", w2_raw[:], M)
+        w_q[1] = quantize("w2", w2_bf, M)
+        for g in range(G):
+            z_product(0, g, 1)
+        wo_bf = interleave(nc.vector.tensor_copy, "wo", wo_raw[:], M)
         x_bf[1] = interleave(nc.vector.tensor_copy, "x1", x1_raw[:], widths[1])
         wo_q = quantize("wo", wo_bf, M)
         x_q[1] = quantize("x1", x_bf[1], widths[1])
@@ -123,8 +129,6 @@ def tile_rows_bgaussshare_kernel(tc, x, w1, w2, fl, wo, dy, old, out):
 
         units = [(c, g) for c in range(3) for g in range(G)]
         squares = {}
-        bells = {}
-        bell_sum = [sb.tile([P, N], F32, name="bell_sum%d" % g) for g in range(G)]
         e1z1 = [sb.tile([P, N], F32, name="e1z1_%d" % g) for g in range(G)]
         az2 = [sb.tile([P, N], F32, name="az2_%d" % g) for g in range(G)]
         az2c = [sb.tile([P, N], F32, name="az2c_%d" % g) for g in range(G)]
@@ -136,25 +140,58 @@ def tile_rows_bgaussshare_kernel(tc, x, w1, w2, fl, wo, dy, old, out):
             squares[u] = sb.tile([P, 2 * w], F32, name="sq%d" % u)
             nc.scalar.activation(out=squares[u][:], in_=banks[c % 2][g][:, 0 : 2 * w], func=ACT.Square)
 
+        bells_all = sb.tile([P, G, 2, N], F32, name="bells")
+        bells = [bells_all[:, g] for g in range(G)]
+
         def bell(u):
+            c, g = units[u]
+            nc.scalar.activation(
+                out=bells[g][:, :, chunks[c]],
+                in_=squares[u][:].rearrange("p (s w) -> p s w", s=2),
+                func=ACT.Exp,
+                scale=-1.0,
+            )
+
+        def first_bells(s):
+            nc.scalar.activation(
+                out=bells_all[:, :, s, chunks[0]], in_=first_squares[:, :, s], func=ACT.Exp, scale=-1.0
+            )
+
+        def times_z2(u):
             c, g = units[u]
             w = widths[c]
             z = banks[c % 2][g]
-            bells[u] = sb.tile([P, 2 * w], F32, name="bell%d" % u)
-            nc.scalar.activation(out=bells[u][:], in_=squares[u][:], func=ACT.Exp, scale=-1.0)
-            nc.gpsimd.tensor_tensor(
-                out=bell_sum[g][:, chunks[c]], in0=bells[u][:, 0:w], in1=bells[u][:, w:], op=ALU.add
-            )
-            nc.vector.tensor_tensor(
-                out=e1z1[g][:, chunks[c]], in0=z[:, 0:w], in1=bells[u][:, 0:w], op=ALU.mult
-            )
             nc.vector.scalar_tensor_tensor(
                 out=az2[g][:, chunks[c]],
-                in0=bells[u][:, w:],
+                in0=bells[g][:, 1, chunks[c]],
                 scalar=floor[g],
                 in1=z[:, w : 2 * w],
                 op0=ALU.add,
                 op1=ALU.mult,
+            )
+
+        def times_z1(u):
+            c, g = units[u]
+            w = widths[c]
+            z = banks[c % 2][g]
+            nc.vector.tensor_tensor(
+                out=e1z1[g][:, chunks[c]], in0=z[:, 0:w], in1=bells[g][:, 0, chunks[c]], op=ALU.mult
+            )
+
+        def times_z(u):
+            times_z2(u)
+            times_z1(u)
+
+        bell_sum = {}
+
+        def add_bells(gs, cols):
+            if not bell_sum:
+                sums = sb.tile([P, G, N], F32, name="bell_sum", tag="dy_bf1", align_bytes=64)
+                bell_sum["all"] = sums
+                for g in range(G):
+                    bell_sum[g] = sums[:, g]
+            nc.gpsimd.tensor_tensor(
+                out=bell_sum["all"][:, gs, cols], in0=bells_all[:, gs, 0, cols], in1=bells_all[:, gs, 1, cols], op=ALU.add
             )
 
         dy_bf = {}
@@ -167,7 +204,7 @@ def tile_rows_bgaussshare_kernel(tc, x, w1, w2, fl, wo, dy, old, out):
             x_q[2] = quantize("x2", x_bf[2], widths[2])
 
         def dy_copy(h):
-            dy_bf[h] = interleave(nc.vector.tensor_copy, "dy%d" % h, dy_raw[:, :, halves[h]], HALF)
+            dy_bf[h] = interleave(nc.vector.tensor_copy, "dy%d" % h, dy_raw[h][:], HALF, "dy_bf%d" % h)
 
         def dy_quant(h):
             dy_q[h] = quantize("dy%d" % h, dy_bf[h], HALF)
@@ -184,30 +221,40 @@ def tile_rows_bgaussshare_kernel(tc, x, w1, w2, fl, wo, dy, old, out):
         def numerator(engine, g, cols):
             engine.tensor_tensor(out=numer[g][:, cols], in0=az2c[g][:, cols], in1=e1z1[g][:, cols], op=ALU.mult)
 
-        extra = {
-            0: [x2_copy],
-            1: [x2_quant] + [lambda: z_products(2, 0), lambda: z_products(2, 1)],
-            2: [lambda: z_products(2, 2)],
-            3: [lambda: z_products(2, 3)],
-            5: [lambda: dy_copy(0)],
-            7: [lambda: dy_copy(1)],
-            8: [lambda: dy_quant(0), lambda: dy_quant(1)] + [lambda g=g: c_products(g) for g in range(G)],
-            10: [lambda: times_c0(0)],
-        }
-        square(0)
-        for u in range(len(units)):
+        def scalar_step(u):
             if u + 1 < len(units):
                 square(u + 1)
             bell(u)
-            for f in extra.get(u, []):
-                f()
-        numerator(nc.gpsimd, 0, whole)
-        times_c0(1)
-        numerator(nc.gpsimd, 1, halves[0])
-        times_c0(2)
-        times_c0(3)
-        numerator(nc.vector, 1, halves[1])
-        numerator(nc.vector, 2, whole)
+
+        first_square(0, 1)
+        first_bells(0)
+        for g in (1, 2, 3):
+            first_square(g, 1)
+        square(4)
+        first_bells(1)
+        for g in range(G):
+            times_z1(g)
+        x2_copy()
+        times_z2(0)
+        x2_quant()
+        z_products(2, 0)
+        for g in (1, 2, 3):
+            times_z2(g)
+            z_products(2, g)
+        for u in (4, 5, 6, 7):
+            scalar_step(u)
+        dy_copy(0)
+        dy_copy(1)
+        dy_quant(0)
+        dy_quant(1)
+        for g in range(G):
+            times_z(4 + g)
+            c_products(g)
+        for g in range(G):
+            scalar_step(8 + g)
+            add_bells(slice(g, g + 1), whole)
+            times_z(8 + g)
+            times_c0(g)
 
         s2 = {}
         rinv = {}
@@ -247,35 +294,38 @@ def tile_rows_bgaussshare_kernel(tc, x, w1, w2, fl, wo, dy, old, out):
 
         def finish(g, cols):
             nc.vector.tensor_tensor(out=res[g][:, cols], in0=prod[g][:, cols], in1=old_sb[:, g, cols], op=ALU.add)
+
+        def store(g, cols):
             nc.sync.dma_start(out=out[g, :, cols], in_=res[g][:, cols])
 
         a, b = halves
         sum_square(0, whole)
         inv(0, whole)
         sum_square(1, whole)
+        inv_square(0, whole)
         inv(1, whole)
         sum_square(2, whole)
         inv_square(1, whole)
-        inv(2, a)
-        inv(2, b)
-        inv_square(2, a)
-        sum_square(3, a)
-        inv_square(2, b)
-        inv(3, a)
-        sum_square(3, b)
-        inv_square(3, a)
-        inv(3, b)
-        inv_square(3, b)
-        scale_inv(0, whole)
+        for g in (2, 3):
+            if g == 3:
+                sum_square(g, a)
+                sum_square(g, b)
+            inv(g, a)
+            inv(g, b)
+            inv_square(g, a)
+            inv_square(g, b)
+        numerator(nc.vector, 0, whole)
+        numerator(nc.vector, 1, whole)
+        numerator(nc.vector, 2, whole)
+        scale(0, whole)
         numerator(nc.vector, 3, whole)
-        scale_again(0, whole)
-        scale(1, whole)
         finish(0, whole)
-        finish(1, whole)
-        scale(2, a)
-        scale(2, b)
-        finish(2, whole)
-        scale(3, a)
-        finish(3, a)
-        scale(3, b)
-        finish(3, b)
+        store(0, whole)
+        for g in (1, 2, 3):
+            scale(g, a)
+            scale(g, b)
+            finish(g, a)
+            if g == 3:
+                store(g, a)
+            finish(g, b)
+            store(g, b if g == 3 else whole)

from contextlib import ExitStack

import concourse.mybir as mybir

G, D, M, N = 4, 128, 128, 512
FLOPS = 3 * 2 * G * D * M * N

F32 = mybir.dt.float32
BF16 = mybir.dt.bfloat16
U32 = mybir.dt.uint32
U8 = mybir.dt.uint8
FP8X4 = mybir.dt.float8_e4m3fn_x4
ACT = mybir.ActivationFunctionType
ALU = mybir.AluOpType

P = 128
PACK = 4
ROWS = D // PACK
HALF = N // 2
MM_N = 128


def tile_rows_bgaussshare_kernel(tc, x, w1, w2, fl, wo, dy, old, out):
    nc = tc.nc

    with ExitStack() as ctx:
        sb = ctx.enter_context(tc.tile_pool(name="sb", bufs=1))
        ps = ctx.enter_context(tc.psum_pool(name="ps", bufs=1))
        ctx.enter_context(tc.manual_schedule())

        def by_partition(a):
            return a.rearrange("g d n -> (g d) n").rearrange("(q j) n -> q j n", j=PACK)

        def load(name, src, width):
            raw = sb.tile([P, PACK, width], F32, name=name + "_raw")
            nc.sync.dma_start(out=raw[:], in_=src)
            return raw

        def interleave(copy, name, raw_ap, width, tag=""):
            packed = sb.tile([P, width, PACK], BF16, name=name + "_bf", tag=tag, align_bytes=64)
            copy(
                out=packed[:].rearrange("p (c i) t -> p c t i", i=4),
                in_=raw_ap.rearrange("p t (c i) -> p c t i", i=4),
            )
            return packed

        def quantize(name, packed, width):
            codes = sb.tile([P, width], U32, name=name + "_codes", align_bytes=64)
            scales = sb.tile([P, width], U8, name=name + "_scales", align_bytes=64)
            nc.vector.quantize_mx(
                out=codes[:].bitcast(FP8X4),
                scales=scales[:],
                in_=packed[:].rearrange("p w j -> p (w j)"),
            )
            return codes, scales

        def product(dst, g, weights, moving, width):
            rows = slice(ROWS * g, ROWS * (g + 1))
            for c in range(width // MM_N):
                cols = slice(MM_N * c, MM_N * (c + 1))
                nc.tensor.matmul_mx(
                    out=dst[:, cols],
                    lhsT=weights[0][rows, :].bitcast(FP8X4),
                    lhsT_scale=weights[1][rows, :],
                    rhs=moving[0][rows, cols].bitcast(FP8X4),
                    rhs_scale=moving[1][rows, cols],
                    start=True,
                    stop=True,
                )

        halves = [slice(0, HALF), slice(HALF, N)]
        whole = slice(0, N)
        chunks = [slice(0, 128), slice(128, 256), slice(256, 512)]
        widths = [c.stop - c.start for c in chunks]
        banks = [[ps.tile([P, N], F32, name="bank%d_%d" % (b, g)) for g in range(G)] for b in range(2)]
        c_bank = banks[1]

        fl_sb = sb.tile([P, G, 8], F32, name="fl_sb")
        nc.scalar.dma_start(out=fl_sb[:, :, 0:1], in_=fl.rearrange("g m o -> m g o"))

        x_hbm = by_partition(x)
        x0_raw = load("x0", x_hbm[:, :, chunks[0]], widths[0])
        w1_raw = load("w1", by_partition(w1), M)
        w2_raw = load("w2", by_partition(w2), M)
        wo_raw = load("wo", by_partition(wo), M)
        x1_raw = load("x1", x_hbm[:, :, chunks[1]], widths[1])
        x2_raw = load("x2", x_hbm[:, :, chunks[2]], widths[2])
        dy_hbm = by_partition(dy)
        dy_raw = [load("dy%d" % h, dy_hbm[:, :, halves[h]], HALF) for h in range(2)]
        old_sb = sb.tile([P, G, N], F32, name="old_sb")
        nc.sync.dma_start(out=old_sb[:], in_=old.rearrange("g m n -> m g n"))

        floor = [fl_sb[:, g, 0:1] for g in range(G)]
        x_q = {}
        x_bf = {}

        def z_product(c, g, s):
            w = widths[c]
            product(banks[c % 2][g][:, s * w : (s + 1) * w], g, w_q[s], x_q[c], w)

        def z_products(c, g):
            z_product(c, g, 0)
            z_product(c, g, 1)

        w_q = {}
        first_squares = sb.tile([P, G, 2, widths[0]], F32, name="first_squares")

        def first_square(g, s):
            w = widths[0]
            nc.scalar.activation(out=first_squares[:, g, s], in_=banks[0][g][:, s * w : (s + 1) * w], func=ACT.Square)

        x_bf[0] = interleave(nc.vector.tensor_copy, "x0", x0_raw[:], widths[0])
        w1_bf = interleave(nc.vector.tensor_copy, "w1", w1_raw[:], M)
        x_q[0] = quantize("x0", x_bf[0], widths[0])
        w_q[0] = quantize("w1", w1_bf, M)
        for g in range(G):
            z_product(0, g, 0)
            first_square(g, 0)
        w2_bf = interleave(nc.vector.tensor_copy, "w2", w2_raw[:], M)
        w_q[1] = quantize("w2", w2_bf, M)
        for g in range(G):
            z_product(0, g, 1)
        wo_bf = interleave(nc.vector.tensor_copy, "wo", wo_raw[:], M)
        x_bf[1] = interleave(nc.vector.tensor_copy, "x1", x1_raw[:], widths[1])
        wo_q = quantize("wo", wo_bf, M)
        x_q[1] = quantize("x1", x_bf[1], widths[1])
        for g in range(G):
            z_products(1, g)

        units = [(c, g) for c in range(3) for g in range(G)]
        squares = {}
        e1z1 = [sb.tile([P, N], F32, name="e1z1_%d" % g) for g in range(G)]
        az2 = [sb.tile([P, N], F32, name="az2_%d" % g) for g in range(G)]
        az2c = [sb.tile([P, N], F32, name="az2c_%d" % g) for g in range(G)]
        numer = [sb.tile([P, N], F32, name="numer%d" % g) for g in range(G)]

        def square(u):
            c, g = units[u]
            w = widths[c]
            squares[u] = sb.tile([P, 2 * w], F32, name="sq%d" % u)
            nc.scalar.activation(out=squares[u][:], in_=banks[c % 2][g][:, 0 : 2 * w], func=ACT.Square)

        bells_all = sb.tile([P, G, 2, N], F32, name="bells")
        bells = [bells_all[:, g] for g in range(G)]

        def bell(u):
            c, g = units[u]
            nc.scalar.activation(
                out=bells[g][:, :, chunks[c]],
                in_=squares[u][:].rearrange("p (s w) -> p s w", s=2),
                func=ACT.Exp,
                scale=-1.0,
            )

        def first_bells(s):
            nc.scalar.activation(
                out=bells_all[:, :, s, chunks[0]], in_=first_squares[:, :, s], func=ACT.Exp, scale=-1.0
            )

        def times_z2(u):
            c, g = units[u]
            w = widths[c]
            z = banks[c % 2][g]
            nc.vector.scalar_tensor_tensor(
                out=az2[g][:, chunks[c]],
                in0=bells[g][:, 1, chunks[c]],
                scalar=floor[g],
                in1=z[:, w : 2 * w],
                op0=ALU.add,
                op1=ALU.mult,
            )

        def times_z1(u):
            c, g = units[u]
            w = widths[c]
            z = banks[c % 2][g]
            nc.vector.tensor_tensor(
                out=e1z1[g][:, chunks[c]], in0=z[:, 0:w], in1=bells[g][:, 0, chunks[c]], op=ALU.mult
            )

        def times_z(u):
            times_z2(u)
            times_z1(u)

        bell_sum = {}

        def add_bells(gs, cols):
            if not bell_sum:
                sums = sb.tile([P, G, N], F32, name="bell_sum", tag="dy_bf1", align_bytes=64)
                bell_sum["all"] = sums
                for g in range(G):
                    bell_sum[g] = sums[:, g]
            nc.gpsimd.tensor_tensor(
                out=bell_sum["all"][:, gs, cols], in0=bells_all[:, gs, 0, cols], in1=bells_all[:, gs, 1, cols], op=ALU.add
            )

        dy_bf = {}
        dy_q = {}

        def x2_copy():
            x_bf[2] = interleave(nc.vector.tensor_copy, "x2", x2_raw[:], widths[2])

        def x2_quant():
            x_q[2] = quantize("x2", x_bf[2], widths[2])

        def dy_copy(h):
            dy_bf[h] = interleave(nc.vector.tensor_copy, "dy%d" % h, dy_raw[h][:], HALF, "dy_bf%d" % h)

        def dy_quant(h):
            dy_q[h] = quantize("dy%d" % h, dy_bf[h], HALF)

        def c_products(g):
            for h in range(2):
                product(c_bank[g][:, halves[h]], g, wo_q, dy_q[h], HALF)

        def times_c0(g):
            nc.vector.scalar_tensor_tensor(
                out=az2c[g][:], in0=az2[g][:], scalar=-2.0, in1=c_bank[g][:], op0=ALU.mult, op1=ALU.mult
            )

        def numerator(engine, g, cols):
            engine.tensor_tensor(out=numer[g][:, cols], in0=az2c[g][:, cols], in1=e1z1[g][:, cols], op=ALU.mult)

        def scalar_step(u):
            if u + 1 < len(units):
                square(u + 1)
            bell(u)

        first_square(0, 1)
        first_bells(0)
        for g in (1, 2, 3):
            first_square(g, 1)
        square(4)
        first_bells(1)
        for g in range(G):
            times_z1(g)
        x2_copy()
        times_z2(0)
        x2_quant()
        z_products(2, 0)
        for g in (1, 2, 3):
            times_z2(g)
            z_products(2, g)
        for u in (4, 5, 6, 7):
            scalar_step(u)
        dy_copy(0)
        dy_copy(1)
        dy_quant(0)
        dy_quant(1)
        for g in range(G):
            times_z(4 + g)
            c_products(g)
        for g in range(G):
            scalar_step(8 + g)
            add_bells(slice(g, g + 1), whole)
            times_z(8 + g)
            times_c0(g)

        s2 = {}
        rinv = {}
        rinv2 = {}
        prod = {}
        res = {}
        half_prod = {}

        def sum_square(g, cols):
            if g not in s2:
                s2[g] = sb.tile([P, N], F32, name="s2_%d" % g)
                rinv[g] = sb.tile([P, N], F32, name="rinv%d" % g)
            nc.scalar.activation(out=s2[g][:, cols], in_=bell_sum[g][:, cols], func=ACT.Square, bias=floor[g])

        def inv(g, cols):
            nc.scalar.activation(out=rinv[g][:, cols], in_=s2[g][:, cols], func=ACT.Abs_reciprocal_sqrt)

        def inv_square(g, cols):
            if g not in rinv2:
                rinv2[g] = sb.tile([P, N], F32, name="rinv2_%d" % g)
                prod[g] = sb.tile([P, N], F32, name="prod%d" % g)
                res[g] = sb.tile([P, N], F32, name="res%d" % g)
            nc.scalar.activation(out=rinv2[g][:, cols], in_=rinv[g][:, cols], func=ACT.Square)

        def scale_inv(g, cols):
            if g not in half_prod:
                half_prod[g] = sb.tile([P, N], F32, name="half_prod%d" % g)
                prod[g] = sb.tile([P, N], F32, name="prod%d" % g)
                res[g] = sb.tile([P, N], F32, name="res%d" % g)
            nc.vector.tensor_tensor(out=half_prod[g][:, cols], in0=numer[g][:, cols], in1=rinv[g][:, cols], op=ALU.mult)

        def scale_again(g, cols):
            nc.vector.tensor_tensor(out=prod[g][:, cols], in0=half_prod[g][:, cols], in1=rinv[g][:, cols], op=ALU.mult)

        def scale(g, cols):
            nc.vector.tensor_tensor(out=prod[g][:, cols], in0=numer[g][:, cols], in1=rinv2[g][:, cols], op=ALU.mult)

        def finish(g, cols):
            nc.vector.tensor_tensor(out=res[g][:, cols], in0=prod[g][:, cols], in1=old_sb[:, g, cols], op=ALU.add)

        def store(g, cols):
            nc.sync.dma_start(out=out[g, :, cols], in_=res[g][:, cols])

        a, b = halves
        sum_square(0, whole)
        inv(0, whole)
        sum_square(1, whole)
        inv_square(0, whole)
        inv(1, whole)
        sum_square(2, whole)
        inv_square(1, whole)
        for g in (2, 3):
            if g == 3:
                sum_square(g, a)
                sum_square(g, b)
            inv(g, a)
            inv(g, b)
            inv_square(g, a)
            inv_square(g, b)
        numerator(nc.vector, 0, whole)
        numerator(nc.vector, 1, whole)
        numerator(nc.vector, 2, whole)
        scale(0, whole)
        numerator(nc.vector, 3, whole)
        finish(0, whole)
        store(0, whole)
        for g in (1, 2, 3):
            scale(g, a)
            scale(g, b)
            finish(g, a)
            if g == 3:
                store(g, a)
            finish(g, b)
            store(g, b if g == 3 else whole)
